import numpy as np
import ml_dtypes


def mxq(x, axis, fmt="e4m3"):
    dtype, down = {"e4m3": (ml_dtypes.float8_e4m3fn, 7), "e5m2": (ml_dtypes.float8_e5m2, 14)}[fmt]
    v = np.moveaxis(np.asarray(x, np.float32).astype(ml_dtypes.bfloat16).astype(np.float64), axis, -1)
    blocks = v.reshape(v.shape[:-1] + (-1, 32))
    amax = np.abs(blocks).max(-1, keepdims=True)
    byte = np.maximum(np.where(amax > 0, np.frexp(amax)[1] - 1 + 127, 0) - down, 1)
    scale = np.exp2(byte - 127.0)
    codes = (blocks / scale).astype(np.float32).astype(dtype).astype(np.float64)
    return np.moveaxis((codes * scale).reshape(v.shape), -1, axis)


WIDE = False


def mx_kscale(k, group=512):
    if not WIDE:
        return np.ones(k)
    levels = np.array([10, -10, 5, -5, 0])
    if group != 512:
        return np.exp2(np.random.permutation(np.resize(levels, k // group))).repeat(group)
    if k % 512:
        return np.exp2(np.random.permutation(np.resize(levels, k // 32))).repeat(32)
    a = np.empty((k // 512, 16))
    for p in range(k // 512):
        a[p, :8] = np.random.permutation(np.resize(levels, 8))
        for g in range(8):
            far = levels[np.abs(levels - a[p, g]) >= 10]
            a[p, g + 8] = far[np.random.randint(len(far))]
    return np.exp2(a.ravel()).repeat(32)


def f64(x):
    return np.asarray(x).astype(np.float64)


G, D, M, N = 2, 256, 256, 1024


def setup_inputs():
    n = np.random.standard_normal
    s = mx_kscale(D, 0)[:, None]
    return {
        "x": (n((G, D, N)) * s).astype(np.float32),
        "w": (n((G, D, M)) / np.sqrt(D) / s).astype(np.float32),
        "b": (0.5 * n((G, M, 1))).astype(np.float32),
    }


def reference(x, w, b):
    xq = mxq(f64(x), 1, "e4m3")
    y = mxq(f64(w), 1, "e4m3").transpose(0, 2, 1) @ xq
    y = y + f64(b)
    y = np.maximum(y, 0.0)
    return y

@@ -1,0 +1,141 @@
+from contextlib import ExitStack
+
+import concourse.mybir as mybir
+
+G, D, M, N = 2, 256, 256, 1024
+FLOPS = 2 * G * D * M * N
+
+F32 = mybir.dt.float32
+BF16 = mybir.dt.bfloat16
+U32 = mybir.dt.uint32
+U8 = mybir.dt.uint8
+FP8X4 = mybir.dt.float8_e4m3fn_x4
+ACT = mybir.ActivationFunctionType
+ALU = mybir.AluOpType
+
+P = 128
+PACK = 4
+ROWS = D // PACK
+HALVES = M // P
+N_MM = 128
+CHUNK = 256
+CHUNKS = N // CHUNK
+SUBS = CHUNK // N_MM
+BANK = 512
+LINE = 4
+
+
+def tile_rows_glin_relu_bias_kernel(tc, x, w, b, out):
+    nc = tc.nc
+    x_rows = x.rearrange("g (p j) n -> (g p) j n", j=PACK)
+    w_rows = w.rearrange("g (p j) m -> (g p) j m", j=PACK)
+    b_cols = b.rearrange("g (q h) o -> q g (h o)", h=HALVES)
+    out_rows = out.rearrange("g (q h) n -> q h g n", h=HALVES)
+
+    with ExitStack() as ctx:
+        sb = ctx.enter_context(tc.tile_pool(name="sb", bufs=1))
+        psum = ctx.enter_context(tc.psum_pool(name="psum", bufs=1))
+        ctx.enter_context(tc.manual_schedule())
+
+        w_raw = sb.tile([P, PACK, M], F32, name="w_raw")
+        w_grp = sb.tile([P, HALVES, P, PACK], BF16, name="w_grp", align_bytes=64)
+        w_codes = sb.tile([P, HALVES, P], U32, name="w_codes", align_bytes=64)
+        w_scales = sb.tile([P, HALVES, P], U8, name="w_scales", align_bytes=64)
+        bias = sb.tile([P, G, 8], F32, name="bias")
+        x_raw = [sb.tile([P, PACK, CHUNK], F32, name="x_raw%d" % c) for c in range(CHUNKS)]
+        x_grp = [sb.tile([P, CHUNK, PACK], BF16, name="x_grp%d" % c, align_bytes=64) for c in range(CHUNKS)]
+        x_codes = [sb.tile([P, CHUNK], U32, name="x_codes%d" % c, align_bytes=64) for c in range(CHUNKS)]
+        x_scales = [sb.tile([P, CHUNK], U8, name="x_scales%d" % c, align_bytes=64) for c in range(CHUNKS)]
+        res = [[sb.tile([P, G, CHUNK], F32, name="res%d_%d" % (c, h)) for h in range(HALVES)] for c in range(CHUNKS)]
+        banks = {}
+        for g in range(G):
+            for h in range(HALVES):
+                for par in range(2):
+                    banks[(g, h, par)] = psum.tile([P, BANK], F32, name="acc%d%d%d" % (g, h, par))
+
+        def acc(c, g, h):
+            lo = (c // 2) * CHUNK
+            return banks[(g, h, c % 2)][:, lo:lo + CHUNK]
+
+        nc.sync.dma_start(out=w_raw[:], in_=w_rows)
+        nc.scalar.dma_start(out=bias[:, :, 0:HALVES], in_=b_cols)
+        for c in range(CHUNKS):
+            nc.sync.dma_start(out=x_raw[c][:], in_=x_rows[:, :, c * CHUNK:(c + 1) * CHUNK])
+
+        def copy_on(engine, dst, src):
+            if engine == "v":
+                nc.vector.tensor_copy(out=dst, in_=src)
+            else:
+                nc.scalar.activation(out=dst, in_=src, func=ACT.Copy)
+
+        w_src = w_raw[:].rearrange("p j (q h) -> p h q j", h=HALVES)
+        copy_on("s", w_grp[:, 1], w_src[:, 1])
+        copy_on("v", w_grp[:, 0], w_src[:, 0])
+        for h in range(HALVES):
+            nc.vector.quantize_mx(
+                out=w_codes[:, h, :].bitcast(FP8X4),
+                scales=w_scales[:, h, :],
+                in_=w_grp[:, h].rearrange("p q j -> p (q j)"),
+            )
+
+        def interleave(engine, c, s):
+            cols = slice(s * N_MM, (s + 1) * N_MM)
+            dst = x_grp[c][:, cols, :].rearrange("p (a i) j -> p a j i", i=LINE)
+            src = x_raw[c][:, :, cols].rearrange("p j (a i) -> p a j i", i=LINE)
+            copy_on(engine, dst, src)
+
+        def quantize(c, s):
+            cols = slice(s * N_MM, (s + 1) * N_MM)
+            nc.vector.quantize_mx(
+                out=x_codes[c][:, cols].bitcast(FP8X4),
+                scales=x_scales[c][:, cols],
+                in_=x_grp[c][:, cols, :].rearrange("p n j -> p (n j)"),
+            )
+
+        def multiply(c):
+            for h in range(HALVES):
+                for s in range(SUBS):
+                    cols = slice(s * N_MM, (s + 1) * N_MM)
+                    for g in range(G):
+                        rows = slice(g * ROWS, (g + 1) * ROWS)
+                        nc.tensor.matmul_mx(
+                            out=acc(c, g, h)[:, cols],
+                            lhsT=w_codes[rows, h, :].bitcast(FP8X4),
+                            lhsT_scale=w_scales[rows, h, :],
+                            rhs=x_codes[c][rows, cols].bitcast(FP8X4),
+                            rhs_scale=x_scales[c][rows, cols],
+                            start=True,
+                            stop=True,
+                        )
+
+        def finish(engine, c, g, h):
+            dst = res[c][h][:, g, :]
+            if engine == "v":
+                nc.vector.tensor_scalar(
+                    out=dst, in0=acc(c, g, h), scalar1=bias[:, g, h:h + 1], scalar2=0.0,
+                    op0=ALU.add, op1=ALU.max,
+                )
+            else:
+                nc.scalar.activation(out=dst, in_=acc(c, g, h), func=ACT.Relu, bias=bias[:, g, h:h + 1])
+
+        def store(c, h):
+            nc.sync.dma_start(out=out_rows[:, h, :, c * CHUNK:(c + 1) * CHUNK], in_=res[c][h][:])
+
+        last = CHUNKS - 1
+
+        def prepare(c):
+            interleave("v", c, 0)
+            interleave("s" if c == 0 else "v", c, 1)
+            quantize(c, 0)
+            quantize(c, 1)
+            multiply(c)
+
+        prepare(0)
+        for c in range(CHUNKS):
+            if c < last:
+                prepare(c + 1)
+            for h in range(HALVES):
+                finish("s", c, 0, h)
+                on_vector = c == last or (c == last - 1 and h == 1)
+                finish("v" if on_vector else "s", c, 1, h)
+                store(c, h)

@@ -23,14 +23,15 @@ CHUNKS = N // CHUNK
 SUBS = CHUNK // N_MM
 BANK = 512
 LINE = 4
+QUAD = 32
 
 
 def tile_rows_glin_relu_bias_kernel(tc, x, w, b, out):
     nc = tc.nc
     x_rows = x.rearrange("g (p j) n -> (g p) j n", j=PACK)
     w_rows = w.rearrange("g (p j) m -> (g p) j m", j=PACK)
-    b_cols = b.rearrange("g (q h) o -> q g (h o)", h=HALVES)
-    out_rows = out.rearrange("g (q h) n -> q h g n", h=HALVES)
+    b_rows = b.rearrange("g (h u i) o -> u (g h) (i o)", h=HALVES, i=QUAD)
+    out_rows = out.rearrange("g (h q) n -> q h g n", h=HALVES)
 
     with ExitStack() as ctx:
         sb = ctx.enter_context(tc.tile_pool(name="sb", bufs=1))
@@ -41,7 +42,8 @@ def tile_rows_glin_relu_bias_kernel(tc, x, w, b, out):
         w_grp = sb.tile([P, HALVES, P, PACK], BF16, name="w_grp", align_bytes=64)
         w_codes = sb.tile([P, HALVES, P], U32, name="w_codes", align_bytes=64)
         w_scales = sb.tile([P, HALVES, P], U8, name="w_scales", align_bytes=64)
-        bias = sb.tile([P, G, 8], F32, name="bias")
+        bias_rows = sb.tile([P, G * HALVES, QUAD], F32, name="bias_rows", align_bytes=64)
+        bias = sb.tile([P, G * HALVES, QUAD], F32, name="bias", align_bytes=64)
         x_raw = [sb.tile([P, PACK, CHUNK], F32, name="x_raw%d" % c) for c in range(CHUNKS)]
         x_grp = [sb.tile([P, CHUNK, PACK], BF16, name="x_grp%d" % c, align_bytes=64) for c in range(CHUNKS)]
         x_codes = [sb.tile([P, CHUNK], U32, name="x_codes%d" % c, align_bytes=64) for c in range(CHUNKS)]
@@ -58,7 +60,8 @@ def tile_rows_glin_relu_bias_kernel(tc, x, w, b, out):
             return banks[(g, h, c % 2)][:, lo:lo + CHUNK]
 
         nc.sync.dma_start(out=w_raw[:], in_=w_rows)
-        nc.scalar.dma_start(out=bias[:, :, 0:HALVES], in_=b_cols)
+        nc.vector.memset(bias_rows[:], 0.0)
+        nc.sync.dma_start(out=bias_rows[0:P:QUAD], in_=b_rows)
         for c in range(CHUNKS):
             nc.sync.dma_start(out=x_raw[c][:], in_=x_rows[:, :, c * CHUNK:(c + 1) * CHUNK])
 
@@ -68,9 +71,11 @@ def tile_rows_glin_relu_bias_kernel(tc, x, w, b, out):
             else:
                 nc.scalar.activation(out=dst, in_=src, func=ACT.Copy)
 
-        w_src = w_raw[:].rearrange("p j (q h) -> p h q j", h=HALVES)
-        copy_on("s", w_grp[:, 1], w_src[:, 1])
-        copy_on("v", w_grp[:, 0], w_src[:, 0])
+        w_src = w_raw[:].rearrange("p j (h a i) -> p h a j i", h=HALVES, i=LINE)
+        w_dst = w_grp[:].rearrange("p h (a i) j -> p h a j i", i=LINE)
+        copy_on("s", w_dst[:, 1], w_src[:, 1])
+        copy_on("v", w_dst[:, 0], w_src[:, 0])
+        nc.vector.transpose(out=bias[:].rearrange("p c i -> p (c i)"), in_=bias_rows[:].rearrange("p c i -> p (c i)"))
         for h in range(HALVES):
             nc.vector.quantize_mx(
                 out=w_codes[:, h, :].bitcast(FP8X4),
@@ -112,11 +117,11 @@ def tile_rows_glin_relu_bias_kernel(tc, x, w, b, out):
             dst = res[c][h][:, g, :]
             if engine == "v":
                 nc.vector.tensor_scalar(
-                    out=dst, in0=acc(c, g, h), scalar1=bias[:, g, h:h + 1], scalar2=0.0,
+                    out=dst, in0=acc(c, g, h), scalar1=bias[:, g * HALVES + h, 0:1], scalar2=0.0,
                     op0=ALU.add, op1=ALU.max,
                 )
             else:
-                nc.scalar.activation(out=dst, in_=acc(c, g, h), func=ACT.Relu, bias=bias[:, g, h:h + 1])
+                nc.scalar.activation(out=dst, in_=acc(c, g, h), func=ACT.Relu, bias=bias[:, g * HALVES + h, 0:1])
 
         def store(c, h):
             nc.sync.dma_start(out=out_rows[:, h, :, c * CHUNK:(c + 1) * CHUNK], in_=res[c][h][:])

@@ -48,7 +48,25 @@ def tile_rows_glin_relu_bias_kernel(tc, x, w, b, out):
         x_grp = [sb.tile([P, CHUNK, PACK], BF16, name="x_grp%d" % c, align_bytes=64) for c in range(CHUNKS)]
         x_codes = [sb.tile([P, CHUNK], U32, name="x_codes%d" % c, align_bytes=64) for c in range(CHUNKS)]
         x_scales = [sb.tile([P, CHUNK], U8, name="x_scales%d" % c, align_bytes=64) for c in range(CHUNKS)]
-        res = [[sb.tile([P, G, CHUNK], F32, name="res%d_%d" % (c, h)) for h in range(HALVES)] for c in range(CHUNKS)]
+        pieces = []
+        for h in range(HALVES):
+            c = 0
+            while c < CHUNKS:
+                if c % 2 != h and c + 1 < CHUNKS:
+                    for g in range(G):
+                        pieces.append((h, c, 2, (g,)))
+                    c += 2
+                else:
+                    pieces.append((h, c, 1, tuple(range(G))))
+                    c += 1
+        res = {}
+        home = {}
+        for piece in pieces:
+            h, c0, span, groups = piece
+            res[piece] = sb.tile([P, len(groups), span * CHUNK], F32, name="res%d_%d_%d" % (h, c0, groups[0]))
+            for g in groups:
+                for c in range(c0, c0 + span):
+                    home[(c, g, h)] = piece
         banks = {}
         for g in range(G):
             for h in range(HALVES):
@@ -97,8 +115,11 @@ def tile_rows_glin_relu_bias_kernel(tc, x, w, b, out):
                 in_=x_grp[c][:, cols, :].rearrange("p n j -> p (n j)"),
             )
 
+        def halves(c):
+            return (c % 2, 1 - c % 2)
+
         def multiply(c):
-            for h in range(HALVES):
+            for h in halves(c):
                 for s in range(SUBS):
                     cols = slice(s * N_MM, (s + 1) * N_MM)
                     for g in range(G):
@@ -114,7 +135,9 @@ def tile_rows_glin_relu_bias_kernel(tc, x, w, b, out):
                         )
 
         def finish(engine, c, g, h):
-            dst = res[c][h][:, g, :]
+            piece = home[(c, g, h)]
+            lo = (c - piece[1]) * CHUNK
+            dst = res[piece][:, g - piece[3][0], lo:lo + CHUNK]
             if engine == "v":
                 nc.vector.tensor_scalar(
                     out=dst, in0=acc(c, g, h), scalar1=bias[:, g * HALVES + h, 0:1], scalar2=0.0,
@@ -123,8 +146,12 @@ def tile_rows_glin_relu_bias_kernel(tc, x, w, b, out):
             else:
                 nc.scalar.activation(out=dst, in_=acc(c, g, h), func=ACT.Relu, bias=bias[:, g * HALVES + h, 0:1])
 
-        def store(c, h):
-            nc.sync.dma_start(out=out_rows[:, h, :, c * CHUNK:(c + 1) * CHUNK], in_=res[c][h][:])
+        def store(c, g, h):
+            piece = home[(c, g, h)]
+            c0, span, groups = piece[1:]
+            if c == c0 + span - 1 and g == groups[-1]:
+                cols = slice(c0 * CHUNK, (c0 + span) * CHUNK)
+                nc.sync.dma_start(out=out_rows[:, h, groups[0]:groups[-1] + 1, cols], in_=res[piece][:])
 
         last = CHUNKS - 1
 
@@ -139,8 +166,9 @@ def tile_rows_glin_relu_bias_kernel(tc, x, w, b, out):
         for c in range(CHUNKS):
             if c < last:
                 prepare(c + 1)
-            for h in range(HALVES):
+            for h in halves(c):
                 finish("s", c, 0, h)
-                on_vector = c == last or (c == last - 1 and h == 1)
+                store(c, 0, h)
+                on_vector = c == last or (c == last - 1 and h == halves(c)[1])
                 finish("v" if on_vector else "s", c, 1, h)
-                store(c, h)
+                store(c, 1, h)

@@ -18,11 +18,14 @@ PACK = 4
 ROWS = D // PACK
 HALVES = M // P
 N_MM = 128
-CHUNK = 256
-CHUNKS = N // CHUNK
-SUBS = CHUNK // N_MM
+UNITS = N // N_MM
+SUBS = 2
+STEP = SUBS * N_MM
+STEPS = N // STEP
+LEAD = 0
 BANK = 512
-LINE = 4
+BANKS = 4
+LINE = 2
 QUAD = 32
 
 
@@ -32,6 +35,8 @@ def tile_rows_glin_relu_bias_kernel(tc, x, w, b, out):
     w_rows = w.rearrange("g (p j) m -> (g p) j m", j=PACK)
     b_rows = b.rearrange("g (h u i) o -> u (g h) (i o)", h=HALVES, i=QUAD)
     out_rows = out.rearrange("g (h q) n -> q h g n", h=HALVES)
+    last = STEPS - 1
+    edges = [0] + [k * STEP + LEAD for k in range(1, STEPS)] + [N]
 
     with ExitStack() as ctx:
         sb = ctx.enter_context(tc.tile_pool(name="sb", bufs=1))
@@ -44,44 +49,56 @@ def tile_rows_glin_relu_bias_kernel(tc, x, w, b, out):
         w_scales = sb.tile([P, HALVES, P], U8, name="w_scales", align_bytes=64)
         bias_rows = sb.tile([P, G * HALVES, QUAD], F32, name="bias_rows", align_bytes=64)
         bias = sb.tile([P, G * HALVES, QUAD], F32, name="bias", align_bytes=64)
-        x_raw = [sb.tile([P, PACK, CHUNK], F32, name="x_raw%d" % c) for c in range(CHUNKS)]
-        x_grp = [sb.tile([P, CHUNK, PACK], BF16, name="x_grp%d" % c, align_bytes=64) for c in range(CHUNKS)]
-        x_codes = [sb.tile([P, CHUNK], U32, name="x_codes%d" % c, align_bytes=64) for c in range(CHUNKS)]
-        x_scales = [sb.tile([P, CHUNK], U8, name="x_scales%d" % c, align_bytes=64) for c in range(CHUNKS)]
+        x_raw = [sb.tile([P, PACK, edges[k + 1] - edges[k]], F32, name="x_raw%d" % k) for k in range(STEPS)]
+        x_grp = [sb.tile([P, N_MM, PACK], BF16, name="x_grp%d" % u, align_bytes=64) for u in range(UNITS)]
+        x_codes = [sb.tile([P, N_MM], U32, name="x_codes%d" % u, align_bytes=64) for u in range(UNITS)]
+        x_scales = [sb.tile([P, N_MM], U8, name="x_scales%d" % u, align_bytes=64) for u in range(UNITS)]
+
+        def halves(k):
+            return (k % 2, 1 - k % 2)
+
         pieces = []
         for h in range(HALVES):
-            c = 0
-            while c < CHUNKS:
-                if c % 2 != h and c + 1 < CHUNKS:
+            k = 0
+            while k < STEPS:
+                if k % 2 != h and k + 1 < STEPS:
                     for g in range(G):
-                        pieces.append((h, c, 2, (g,)))
-                    c += 2
+                        pieces.append((h, k, 2, (g,)))
+                    k += 2
                 else:
-                    pieces.append((h, c, 1, tuple(range(G))))
-                    c += 1
+                    pieces.append((h, k, 1, tuple(range(G))))
+                    k += 1
         res = {}
         home = {}
         for piece in pieces:
-            h, c0, span, groups = piece
-            res[piece] = sb.tile([P, len(groups), span * CHUNK], F32, name="res%d_%d_%d" % (h, c0, groups[0]))
+            h, k0, span, groups = piece
+            res[piece] = sb.tile([P, len(groups), span * STEP], F32, name="res%d_%d_%d" % (h, k0, groups[0]))
             for g in groups:
-                for c in range(c0, c0 + span):
-                    home[(c, g, h)] = piece
-        banks = {}
-        for g in range(G):
-            for h in range(HALVES):
-                for par in range(2):
-                    banks[(g, h, par)] = psum.tile([P, BANK], F32, name="acc%d%d%d" % (g, h, par))
+                for k in range(k0, k0 + span):
+                    home[(k, g, h)] = piece
 
-        def acc(c, g, h):
-            lo = (c // 2) * CHUNK
-            return banks[(g, h, c % 2)][:, lo:lo + CHUNK]
+        def by_unit(k, g, h):
+            return h == halves(k)[0] and (g == 0 or k == last)
+
+        banks = [[psum.tile([P, BANK], F32, name="acc%d%d" % (g, i)) for i in range(BANKS)] for g in range(G)]
+        acc = {}
+        for g in range(G):
+            turn = 0
+            for k in range(STEPS):
+                for h in halves(k):
+                    for s in range(SUBS):
+                        acc[(k, g, h, s)] = (banks[g][turn % BANKS], s * N_MM)
+                        if s == SUBS - 1 or by_unit(k, g, h):
+                            turn += 1
+
+        def load(k):
+            nc.sync.dma_start(out=x_raw[k][:], in_=x_rows[:, :, edges[k]:edges[k + 1]])
 
         nc.sync.dma_start(out=w_raw[:], in_=w_rows)
         nc.vector.memset(bias_rows[:], 0.0)
         nc.sync.dma_start(out=bias_rows[0:P:QUAD], in_=b_rows)
-        for c in range(CHUNKS):
-            nc.sync.dma_start(out=x_raw[c][:], in_=x_rows[:, :, c * CHUNK:(c + 1) * CHUNK])
+        for k in range(STEPS):
+            load(k)
 
         def copy_on(engine, dst, src):
             if engine == "v":
@@ -89,86 +106,88 @@ def tile_rows_glin_relu_bias_kernel(tc, x, w, b, out):
             else:
                 nc.scalar.activation(out=dst, in_=src, func=ACT.Copy)
 
-        w_src = w_raw[:].rearrange("p j (h a i) -> p h a j i", h=HALVES, i=LINE)
-        w_dst = w_grp[:].rearrange("p h (a i) j -> p h a j i", i=LINE)
-        copy_on("s", w_dst[:, 1], w_src[:, 1])
-        copy_on("v", w_dst[:, 0], w_src[:, 0])
-        nc.vector.transpose(out=bias[:].rearrange("p c i -> p (c i)"), in_=bias_rows[:].rearrange("p c i -> p (c i)"))
-        for h in range(HALVES):
-            nc.vector.quantize_mx(
-                out=w_codes[:, h, :].bitcast(FP8X4),
-                scales=w_scales[:, h, :],
-                in_=w_grp[:, h].rearrange("p q j -> p (q j)"),
-            )
-
-        def interleave(engine, c, s):
-            cols = slice(s * N_MM, (s + 1) * N_MM)
-            dst = x_grp[c][:, cols, :].rearrange("p (a i) j -> p a j i", i=LINE)
-            src = x_raw[c][:, :, cols].rearrange("p j (a i) -> p a j i", i=LINE)
+        def interleave(engine, k, lo, hi):
+            u = lo // N_MM
+            dst = x_grp[u][:, lo - u * N_MM:hi - u * N_MM, :].rearrange("p (a i) j -> p a j i", i=LINE)
+            src = x_raw[k][:, :, lo - edges[k]:hi - edges[k]].rearrange("p j (a i) -> p a j i", i=LINE)
             copy_on(engine, dst, src)
 
-        def quantize(c, s):
-            cols = slice(s * N_MM, (s + 1) * N_MM)
+        def quantize(u):
             nc.vector.quantize_mx(
-                out=x_codes[c][:, cols].bitcast(FP8X4),
-                scales=x_scales[c][:, cols],
-                in_=x_grp[c][:, cols, :].rearrange("p n j -> p (n j)"),
+                out=x_codes[u][:].bitcast(FP8X4),
+                scales=x_scales[u][:],
+                in_=x_grp[u][:].rearrange("p n j -> p (n j)"),
             )
 
-        def halves(c):
-            return (c % 2, 1 - c % 2)
+        def weights():
+            w_src = w_raw[:].rearrange("p j (h a i) -> p h a j i", h=HALVES, i=LINE)
+            w_dst = w_grp[:].rearrange("p h (a i) j -> p h a j i", i=LINE)
+            copy_on("s", w_dst[:, 1], w_src[:, 1])
+            copy_on("v", w_dst[:, 0], w_src[:, 0])
+            turn_bias()
+            for h in range(HALVES):
+                nc.vector.quantize_mx(
+                    out=w_codes[:, h, :].bitcast(FP8X4),
+                    scales=w_scales[:, h, :],
+                    in_=w_grp[:, h].rearrange("p q j -> p (q j)"),
+                )
 
-        def multiply(c):
-            for h in halves(c):
+        def turn_bias():
+            nc.vector.transpose(out=bias[:].rearrange("p c i -> p (c i)"), in_=bias_rows[:].rearrange("p c i -> p (c i)"))
+
+        def prepare(k):
+            mid = k * STEP + N_MM
+            interleave("v", k, edges[k], mid)
+            interleave("s" if k == 0 else "v", k, mid, mid + N_MM)
+            quantize(SUBS * k)
+            quantize(SUBS * k + 1)
+
+        def multiply(k):
+            for h in halves(k):
                 for s in range(SUBS):
-                    cols = slice(s * N_MM, (s + 1) * N_MM)
+                    u = SUBS * k + s
                     for g in range(G):
                         rows = slice(g * ROWS, (g + 1) * ROWS)
+                        bank, lo = acc[(k, g, h, s)]
                         nc.tensor.matmul_mx(
-                            out=acc(c, g, h)[:, cols],
+                            out=bank[:, lo:lo + N_MM],
                             lhsT=w_codes[rows, h, :].bitcast(FP8X4),
                             lhsT_scale=w_scales[rows, h, :],
-                            rhs=x_codes[c][rows, cols].bitcast(FP8X4),
-                            rhs_scale=x_scales[c][rows, cols],
+                            rhs=x_codes[u][rows, :].bitcast(FP8X4),
+                            rhs_scale=x_scales[u][rows, :],
                             start=True,
                             stop=True,
                         )
 
-        def finish(engine, c, g, h):
-            piece = home[(c, g, h)]
-            lo = (c - piece[1]) * CHUNK
-            dst = res[piece][:, g - piece[3][0], lo:lo + CHUNK]
-            if engine == "v":
-                nc.vector.tensor_scalar(
-                    out=dst, in0=acc(c, g, h), scalar1=bias[:, g * HALVES + h, 0:1], scalar2=0.0,
-                    op0=ALU.add, op1=ALU.max,
-                )
-            else:
-                nc.scalar.activation(out=dst, in_=acc(c, g, h), func=ACT.Relu, bias=bias[:, g * HALVES + h, 0:1])
-
-        def store(c, g, h):
-            piece = home[(c, g, h)]
-            c0, span, groups = piece[1:]
-            if c == c0 + span - 1 and g == groups[-1]:
-                cols = slice(c0 * CHUNK, (c0 + span) * CHUNK)
+        def finish(engine, k, g, h):
+            piece = home[(k, g, h)]
+            k0, span, groups = piece[1:]
+            width = N_MM if by_unit(k, g, h) else STEP
+            for s in range(STEP // width):
+                at = (k - k0) * STEP + s * N_MM
+                dst = res[piece][:, g - groups[0], at:at + width]
+                bank, lo = acc[(k, g, h, s)]
+                src = bank[:, lo:lo + width]
+                if engine == "v":
+                    nc.vector.tensor_scalar(
+                        out=dst, in0=src, scalar1=bias[:, g * HALVES + h, 0:1], scalar2=0.0,
+                        op0=ALU.add, op1=ALU.max,
+                    )
+                else:
+                    nc.scalar.activation(out=dst, in_=src, func=ACT.Relu, bias=bias[:, g * HALVES + h, 0:1])
+            if k == k0 + span - 1 and g == groups[-1]:
+                cols = slice(k0 * STEP, (k0 + span) * STEP)
                 nc.sync.dma_start(out=out_rows[:, h, groups[0]:groups[-1] + 1, cols], in_=res[piece][:])
 
-        last = CHUNKS - 1
-
-        def prepare(c):
-            interleave("v", c, 0)
-            interleave("s" if c == 0 else "v", c, 1)
-            quantize(c, 0)
-            quantize(c, 1)
-            multiply(c)
-
+        weights()
         prepare(0)
-        for c in range(CHUNKS):
-            if c < last:
-                prepare(c + 1)
-            for h in halves(c):
-                finish("s", c, 0, h)
-                store(c, 0, h)
-                on_vector = c == last or (c == last - 1 and h == halves(c)[1])
-                finish("v" if on_vector else "s", c, 1, h)
-                store(c, 1, h)
+        multiply(0)
+        for k in range(STEPS):
+            if k < last:
+                prepare(k + 1)
+            for h in halves(k):
+                finish("s", k, 0, h)
+                on_vector = k == last or (k == last - 1 and h == halves(k)[1])
+                finish("v" if on_vector else "s", k, 1, h)
+            if k < last:
+                multiply(k + 1)

@@ -23,6 +23,7 @@ SUBS = 2
 STEP = SUBS * N_MM
 STEPS = N // STEP
 LEAD = 0
+SHARED = 2
 BANK = 512
 BANKS = 4
 LINE = 2
@@ -43,13 +44,13 @@ def tile_rows_glin_relu_bias_kernel(tc, x, w, b, out):
         psum = ctx.enter_context(tc.psum_pool(name="psum", bufs=1))
         ctx.enter_context(tc.manual_schedule())
 
-        w_raw = sb.tile([P, PACK, M], F32, name="w_raw")
+        w_raw = sb.tile([P, PACK, M], F32, name="w_raw", align_bytes=256)
         w_grp = sb.tile([P, HALVES, P, PACK], BF16, name="w_grp", align_bytes=64)
         w_codes = sb.tile([P, HALVES, P], U32, name="w_codes", align_bytes=64)
         w_scales = sb.tile([P, HALVES, P], U8, name="w_scales", align_bytes=64)
         bias_rows = sb.tile([P, G * HALVES, QUAD], F32, name="bias_rows", align_bytes=64)
         bias = sb.tile([P, G * HALVES, QUAD], F32, name="bias", align_bytes=64)
-        x_raw = [sb.tile([P, PACK, edges[k + 1] - edges[k]], F32, name="x_raw%d" % k) for k in range(STEPS)]
+        x_raw = [sb.tile([P, PACK, edges[k + 1] - edges[k]], F32, name="x_raw%d" % k, align_bytes=256) for k in range(STEPS)]
         x_grp = [sb.tile([P, N_MM, PACK], BF16, name="x_grp%d" % u, align_bytes=64) for u in range(UNITS)]
         x_codes = [sb.tile([P, N_MM], U32, name="x_codes%d" % u, align_bytes=64) for u in range(UNITS)]
         x_scales = [sb.tile([P, N_MM], U8, name="x_scales%d" % u, align_bytes=64) for u in range(UNITS)]
@@ -72,7 +73,7 @@ def tile_rows_glin_relu_bias_kernel(tc, x, w, b, out):
         home = {}
         for piece in pieces:
             h, k0, span, groups = piece
-            res[piece] = sb.tile([P, len(groups), span * STEP], F32, name="res%d_%d_%d" % (h, k0, groups[0]))
+            res[piece] = sb.tile([P, len(groups), span * STEP], F32, name="res%d_%d_%d" % (h, k0, groups[0]), align_bytes=256)
             for g in groups:
                 for k in range(k0, k0 + span):
                     home[(k, g, h)] = piece
@@ -137,8 +138,11 @@ def tile_rows_glin_relu_bias_kernel(tc, x, w, b, out):
 
         def prepare(k):
             mid = k * STEP + N_MM
+            cut = mid + N_MM - (N_MM // 2 if k < SHARED else 0)
             interleave("v", k, edges[k], mid)
-            interleave("s" if k == 0 else "v", k, mid, mid + N_MM)
+            interleave("v", k, mid, cut)
+            if k < SHARED:
+                interleave("s", k, cut, mid + N_MM)
             quantize(SUBS * k)
             quantize(SUBS * k + 1)
 
@@ -185,9 +189,12 @@ def tile_rows_glin_relu_bias_kernel(tc, x, w, b, out):
         for k in range(STEPS):
             if k < last:
                 prepare(k + 1)
-            for h in halves(k):
-                finish("s", k, 0, h)
-                on_vector = k == last or (k == last - 1 and h == halves(k)[1])
-                finish("v" if on_vector else "s", k, 1, h)
+            first, second = halves(k)
+            finish("s", k, 0, first)
+            if k > 0:
+                finish("v" if k == last else "s", k - 1, 1, first)
+            finish("v" if k == last else "s", k, 1, first)
+            finish("s", k, 0, second)
             if k < last:
                 multiply(k + 1)
+        finish("v", last, 1, halves(last)[1])

@@ -18,16 +18,16 @@ PACK = 4
 ROWS = D // PACK
 HALVES = M // P
 N_MM = 128
-UNITS = N // N_MM
-SUBS = 2
-STEP = SUBS * N_MM
+UNITS = 2
+STEP = UNITS * N_MM
 STEPS = N // STEP
-LEAD = 0
-SHARED = 2
 BANK = 512
-BANKS = 4
-LINE = 2
 QUAD = 32
+PAIR = 2
+SHARED = 2
+SHARE = STEP // 4
+MX_ALIGN = 64
+DMA_ALIGN = 512
 
 
 def tile_rows_glin_relu_bias_kernel(tc, x, w, b, out):
@@ -37,124 +37,82 @@ def tile_rows_glin_relu_bias_kernel(tc, x, w, b, out):
     b_rows = b.rearrange("g (h u i) o -> u (g h) (i o)", h=HALVES, i=QUAD)
     out_rows = out.rearrange("g (h q) n -> q h g n", h=HALVES)
     last = STEPS - 1
-    edges = [0] + [k * STEP + LEAD for k in range(1, STEPS)] + [N]
 
     with ExitStack() as ctx:
         sb = ctx.enter_context(tc.tile_pool(name="sb", bufs=1))
         psum = ctx.enter_context(tc.psum_pool(name="psum", bufs=1))
         ctx.enter_context(tc.manual_schedule())
 
-        w_raw = sb.tile([P, PACK, M], F32, name="w_raw", align_bytes=256)
-        w_grp = sb.tile([P, HALVES, P, PACK], BF16, name="w_grp", align_bytes=64)
-        w_codes = sb.tile([P, HALVES, P], U32, name="w_codes", align_bytes=64)
-        w_scales = sb.tile([P, HALVES, P], U8, name="w_scales", align_bytes=64)
-        bias_rows = sb.tile([P, G * HALVES, QUAD], F32, name="bias_rows", align_bytes=64)
-        bias = sb.tile([P, G * HALVES, QUAD], F32, name="bias", align_bytes=64)
-        x_raw = [sb.tile([P, PACK, edges[k + 1] - edges[k]], F32, name="x_raw%d" % k, align_bytes=256) for k in range(STEPS)]
-        x_grp = [sb.tile([P, N_MM, PACK], BF16, name="x_grp%d" % u, align_bytes=64) for u in range(UNITS)]
-        x_codes = [sb.tile([P, N_MM], U32, name="x_codes%d" % u, align_bytes=64) for u in range(UNITS)]
-        x_scales = [sb.tile([P, N_MM], U8, name="x_scales%d" % u, align_bytes=64) for u in range(UNITS)]
-
-        def halves(k):
-            return (k % 2, 1 - k % 2)
-
-        pieces = []
-        for h in range(HALVES):
-            k = 0
-            while k < STEPS:
-                if k % 2 != h and k + 1 < STEPS:
-                    for g in range(G):
-                        pieces.append((h, k, 2, (g,)))
-                    k += 2
-                else:
-                    pieces.append((h, k, 1, tuple(range(G))))
-                    k += 1
+        w_raw = sb.tile([P, PACK, M], F32, name="w_raw", align_bytes=DMA_ALIGN)
+        w_grp = sb.tile([P, HALVES, P, PACK], BF16, name="w_grp", align_bytes=MX_ALIGN)
+        w_codes = sb.tile([P, HALVES, P], U32, name="w_codes", align_bytes=MX_ALIGN)
+        w_scales = sb.tile([P, HALVES, P], U8, name="w_scales", align_bytes=MX_ALIGN)
+        bias_rows = sb.tile([P, G * HALVES, QUAD], F32, name="bias_rows", align_bytes=MX_ALIGN)
+        bias = sb.tile([P, G * HALVES, QUAD], F32, name="bias", align_bytes=MX_ALIGN)
+        x_raw = [sb.tile([P, PACK, STEP], F32, name="x_raw%d" % k, align_bytes=DMA_ALIGN) for k in range(STEPS)]
+        units = range(STEPS * UNITS)
+        x_grp = [sb.tile([P, N_MM, PACK], BF16, name="x_grp%d" % u, align_bytes=MX_ALIGN) for u in units]
+        x_codes = [sb.tile([P, N_MM], U32, name="x_codes%d" % u, align_bytes=MX_ALIGN) for u in units]
+        x_scales = [sb.tile([P, N_MM], U8, name="x_scales%d" % u, align_bytes=MX_ALIGN) for u in units]
         res = {}
-        home = {}
-        for piece in pieces:
-            h, k0, span, groups = piece
-            res[piece] = sb.tile([P, len(groups), span * STEP], F32, name="res%d_%d_%d" % (h, k0, groups[0]), align_bytes=256)
-            for g in groups:
-                for k in range(k0, k0 + span):
-                    home[(k, g, h)] = piece
-
-        def by_unit(k, g, h):
-            return h == halves(k)[0] and (g == 0 or k == last)
-
-        banks = [[psum.tile([P, BANK], F32, name="acc%d%d" % (g, i)) for i in range(BANKS)] for g in range(G)]
-        acc = {}
+        for k in range(STEPS):
+            for h in range(HALVES):
+                res[(k, h)] = sb.tile([P, G, STEP], F32, name="res%d%d" % (k, h), align_bytes=DMA_ALIGN)
+        banks = {}
         for g in range(G):
-            turn = 0
-            for k in range(STEPS):
-                for h in halves(k):
-                    for s in range(SUBS):
-                        acc[(k, g, h, s)] = (banks[g][turn % BANKS], s * N_MM)
-                        if s == SUBS - 1 or by_unit(k, g, h):
-                            turn += 1
+            for h in range(HALVES):
+                for parity in range(2):
+                    banks[(g, h, parity)] = psum.tile([P, BANK], F32, name="acc%d%d%d" % (g, h, parity))
 
-        def load(k):
-            nc.sync.dma_start(out=x_raw[k][:], in_=x_rows[:, :, edges[k]:edges[k + 1]])
+        def acc(k, g, h):
+            lo = (k // 2) * STEP
+            return banks[(g, h, k % 2)][:, lo:lo + STEP]
 
         nc.sync.dma_start(out=w_raw[:], in_=w_rows)
         nc.vector.memset(bias_rows[:], 0.0)
         nc.sync.dma_start(out=bias_rows[0:P:QUAD], in_=b_rows)
         for k in range(STEPS):
-            load(k)
+            nc.sync.dma_start(out=x_raw[k][:], in_=x_rows[:, :, k * STEP:(k + 1) * STEP])
 
-        def copy_on(engine, dst, src):
-            if engine == "v":
+        def interleave(engine, dst, src):
+            dst = dst.rearrange("p (a i) j -> p a j i", i=PAIR)
+            src = src.rearrange("p j (a i) -> p a j i", i=PAIR)
+            if engine == "vector":
                 nc.vector.tensor_copy(out=dst, in_=src)
             else:
                 nc.scalar.activation(out=dst, in_=src, func=ACT.Copy)
 
-        def interleave(engine, k, lo, hi):
-            u = lo // N_MM
-            dst = x_grp[u][:, lo - u * N_MM:hi - u * N_MM, :].rearrange("p (a i) j -> p a j i", i=LINE)
-            src = x_raw[k][:, :, lo - edges[k]:hi - edges[k]].rearrange("p j (a i) -> p a j i", i=LINE)
-            copy_on(engine, dst, src)
-
-        def quantize(u):
+        def quantize(codes, scales, grouped):
             nc.vector.quantize_mx(
-                out=x_codes[u][:].bitcast(FP8X4),
-                scales=x_scales[u][:],
-                in_=x_grp[u][:].rearrange("p n j -> p (n j)"),
+                out=codes.bitcast(FP8X4), scales=scales, in_=grouped.rearrange("p n j -> p (n j)")
             )
 
-        def weights():
-            w_src = w_raw[:].rearrange("p j (h a i) -> p h a j i", h=HALVES, i=LINE)
-            w_dst = w_grp[:].rearrange("p h (a i) j -> p h a j i", i=LINE)
-            copy_on("s", w_dst[:, 1], w_src[:, 1])
-            copy_on("v", w_dst[:, 0], w_src[:, 0])
-            turn_bias()
-            for h in range(HALVES):
-                nc.vector.quantize_mx(
-                    out=w_codes[:, h, :].bitcast(FP8X4),
-                    scales=w_scales[:, h, :],
-                    in_=w_grp[:, h].rearrange("p q j -> p (q j)"),
-                )
-
-        def turn_bias():
-            nc.vector.transpose(out=bias[:].rearrange("p c i -> p (c i)"), in_=bias_rows[:].rearrange("p c i -> p (c i)"))
+        interleave("scalar", w_grp[:, 1], w_raw[:, :, P:M])
+        interleave("vector", w_grp[:, 0], w_raw[:, :, 0:P])
+        nc.vector.transpose(
+            out=bias[:].rearrange("p c i -> p (c i)"), in_=bias_rows[:].rearrange("p c i -> p (c i)")
+        )
+        for h in range(HALVES):
+            quantize(w_codes[:, h, :], w_scales[:, h, :], w_grp[:, h])
 
         def prepare(k):
-            mid = k * STEP + N_MM
-            cut = mid + N_MM - (N_MM // 2 if k < SHARED else 0)
-            interleave("v", k, edges[k], mid)
-            interleave("v", k, mid, cut)
+            early, late = UNITS * k, UNITS * k + 1
+            cut = N_MM - SHARE if k < SHARED else N_MM
+            interleave("vector", x_grp[early][:], x_raw[k][:, :, 0:N_MM])
+            interleave("vector", x_grp[late][:, 0:cut, :], x_raw[k][:, :, N_MM:N_MM + cut])
             if k < SHARED:
-                interleave("s", k, cut, mid + N_MM)
-            quantize(SUBS * k)
-            quantize(SUBS * k + 1)
+                interleave("scalar", x_grp[late][:, cut:N_MM, :], x_raw[k][:, :, N_MM + cut:STEP])
+            for u in (early, late):
+                quantize(x_codes[u][:], x_scales[u][:], x_grp[u][:])
 
         def multiply(k):
-            for h in halves(k):
-                for s in range(SUBS):
-                    u = SUBS * k + s
+            for h in range(HALVES):
+                for s in range(UNITS):
+                    u = UNITS * k + s
                     for g in range(G):
                         rows = slice(g * ROWS, (g + 1) * ROWS)
-                        bank, lo = acc[(k, g, h, s)]
                         nc.tensor.matmul_mx(
-                            out=bank[:, lo:lo + N_MM],
+                            out=acc(k, g, h)[:, s * N_MM:(s + 1) * N_MM],
                             lhsT=w_codes[rows, h, :].bitcast(FP8X4),
                             lhsT_scale=w_scales[rows, h, :],
                             rhs=x_codes[u][rows, :].bitcast(FP8X4),
@@ -164,37 +122,29 @@ def tile_rows_glin_relu_bias_kernel(tc, x, w, b, out):
                         )
 
         def finish(engine, k, g, h):
-            piece = home[(k, g, h)]
-            k0, span, groups = piece[1:]
-            width = N_MM if by_unit(k, g, h) else STEP
-            for s in range(STEP // width):
-                at = (k - k0) * STEP + s * N_MM
-                dst = res[piece][:, g - groups[0], at:at + width]
-                bank, lo = acc[(k, g, h, s)]
-                src = bank[:, lo:lo + width]
-                if engine == "v":
-                    nc.vector.tensor_scalar(
-                        out=dst, in0=src, scalar1=bias[:, g * HALVES + h, 0:1], scalar2=0.0,
-                        op0=ALU.add, op1=ALU.max,
-                    )
-                else:
-                    nc.scalar.activation(out=dst, in_=src, func=ACT.Relu, bias=bias[:, g * HALVES + h, 0:1])
-            if k == k0 + span - 1 and g == groups[-1]:
-                cols = slice(k0 * STEP, (k0 + span) * STEP)
-                nc.sync.dma_start(out=out_rows[:, h, groups[0]:groups[-1] + 1, cols], in_=res[piece][:])
+            column = bias[:, g * HALVES + h, 0:1]
+            if engine == "vector":
+                nc.vector.tensor_scalar(
+                    out=res[(k, h)][:, g], in0=acc(k, g, h), scalar1=column, scalar2=0.0, op0=ALU.add, op1=ALU.max
+                )
+            else:
+                nc.scalar.activation(out=res[(k, h)][:, g], in_=acc(k, g, h), func=ACT.Relu, bias=column)
 
-        weights()
+        def store(k, h, lo, hi):
+            nc.sync.dma_start(out=out_rows[:, h, lo:hi, k * STEP:(k + 1) * STEP], in_=res[(k, h)][:, lo:hi])
+
         prepare(0)
         multiply(0)
         for k in range(STEPS):
             if k < last:
                 prepare(k + 1)
-            first, second = halves(k)
-            finish("s", k, 0, first)
-            if k > 0:
-                finish("v" if k == last else "s", k - 1, 1, first)
-            finish("v" if k == last else "s", k, 1, first)
-            finish("s", k, 0, second)
+            for h in range(HALVES):
+                vector_free = k == last or (k == last - 1 and h == HALVES - 1)
+                finish("scalar", k, 0, h)
+                apart = k == 0 and h == 0
+                if apart:
+                    store(k, h, 0, 1)
+                finish("vector" if vector_free else "scalar", k, 1, h)
+                store(k, h, 1 if apart else 0, G)
             if k < last:
                 multiply(k + 1)
-        finish("v", last, 1, halves(last)[1])

@@ -23,11 +23,13 @@ STEP = UNITS * N_MM
 STEPS = N // STEP
 BANK = 512
 QUAD = 32
+BIAS_STEP = QUAD // (G * HALVES)
 PAIR = 2
-SHARED = 2
-SHARE = STEP // 4
+SHARED = 3
+SHARE = 40
 MX_ALIGN = 64
-DMA_ALIGN = 512
+ROW_ALIGN = STEP * 4
+W_ALIGN = PACK * M * 4
 
 
 def tile_rows_glin_relu_bias_kernel(tc, x, w, b, out):
@@ -43,13 +45,13 @@ def tile_rows_glin_relu_bias_kernel(tc, x, w, b, out):
         psum = ctx.enter_context(tc.psum_pool(name="psum", bufs=1))
         ctx.enter_context(tc.manual_schedule())
 
-        w_raw = sb.tile([P, PACK, M], F32, name="w_raw", align_bytes=DMA_ALIGN)
+        w_raw = sb.tile([P, PACK, M], F32, name="w_raw", align_bytes=W_ALIGN)
         w_grp = sb.tile([P, HALVES, P, PACK], BF16, name="w_grp", align_bytes=MX_ALIGN)
         w_codes = sb.tile([P, HALVES, P], U32, name="w_codes", align_bytes=MX_ALIGN)
         w_scales = sb.tile([P, HALVES, P], U8, name="w_scales", align_bytes=MX_ALIGN)
-        bias_rows = sb.tile([P, G * HALVES, QUAD], F32, name="bias_rows", align_bytes=MX_ALIGN)
-        bias = sb.tile([P, G * HALVES, QUAD], F32, name="bias", align_bytes=MX_ALIGN)
-        x_raw = [sb.tile([P, PACK, STEP], F32, name="x_raw%d" % k, align_bytes=DMA_ALIGN) for k in range(STEPS)]
+        bias_rows = sb.tile([P, QUAD], F32, name="bias_rows", align_bytes=MX_ALIGN)
+        bias = sb.tile([P, QUAD], F32, name="bias", align_bytes=MX_ALIGN)
+        x_raw = [sb.tile([P, PACK, STEP], F32, name="x_raw%d" % k, align_bytes=ROW_ALIGN) for k in range(STEPS)]
         units = range(STEPS * UNITS)
         x_grp = [sb.tile([P, N_MM, PACK], BF16, name="x_grp%d" % u, align_bytes=MX_ALIGN) for u in units]
         x_codes = [sb.tile([P, N_MM], U32, name="x_codes%d" % u, align_bytes=MX_ALIGN) for u in units]
@@ -57,22 +59,25 @@ def tile_rows_glin_relu_bias_kernel(tc, x, w, b, out):
         res = {}
         for k in range(STEPS):
             for h in range(HALVES):
-                res[(k, h)] = sb.tile([P, G, STEP], F32, name="res%d%d" % (k, h), align_bytes=DMA_ALIGN)
+                res[(k, h)] = sb.tile([P, G, STEP], F32, name="res%d%d" % (k, h), align_bytes=ROW_ALIGN)
         banks = {}
         for g in range(G):
             for h in range(HALVES):
                 for parity in range(2):
                     banks[(g, h, parity)] = psum.tile([P, BANK], F32, name="acc%d%d%d" % (g, h, parity))
 
-        def acc(k, g, h):
-            lo = (k // 2) * STEP
-            return banks[(g, h, k % 2)][:, lo:lo + STEP]
+        def acc(k, g, h, s):
+            if g == 0 and h == 0:
+                return banks[(g, h, s)][:, k * N_MM:(k + 1) * N_MM]
+            lo = (k // 2) * STEP + s * N_MM
+            return banks[(g, h, k % 2)][:, lo:lo + N_MM]
 
-        nc.sync.dma_start(out=w_raw[:], in_=w_rows)
         nc.vector.memset(bias_rows[:], 0.0)
-        nc.sync.dma_start(out=bias_rows[0:P:QUAD], in_=b_rows)
+        nc.sync.dma_start(out=w_raw[:], in_=w_rows)
         for k in range(STEPS):
             nc.sync.dma_start(out=x_raw[k][:], in_=x_rows[:, :, k * STEP:(k + 1) * STEP])
+            if k == 0:
+                nc.sync.dma_start(out=bias_rows[0:P:BIAS_STEP], in_=b_rows)
 
         def interleave(engine, dst, src):
             dst = dst.rearrange("p (a i) j -> p a j i", i=PAIR)
@@ -89,20 +94,18 @@ def tile_rows_glin_relu_bias_kernel(tc, x, w, b, out):
 
         interleave("scalar", w_grp[:, 1], w_raw[:, :, P:M])
         interleave("vector", w_grp[:, 0], w_raw[:, :, 0:P])
-        nc.vector.transpose(
-            out=bias[:].rearrange("p c i -> p (c i)"), in_=bias_rows[:].rearrange("p c i -> p (c i)")
-        )
         for h in range(HALVES):
             quantize(w_codes[:, h, :], w_scales[:, h, :], w_grp[:, h])
 
         def prepare(k):
-            early, late = UNITS * k, UNITS * k + 1
-            cut = N_MM - SHARE if k < SHARED else N_MM
-            interleave("vector", x_grp[early][:], x_raw[k][:, :, 0:N_MM])
-            interleave("vector", x_grp[late][:, 0:cut, :], x_raw[k][:, :, N_MM:N_MM + cut])
-            if k < SHARED:
-                interleave("scalar", x_grp[late][:, cut:N_MM, :], x_raw[k][:, :, N_MM + cut:STEP])
-            for u in (early, late):
+            for s in range(UNITS):
+                u, lo = UNITS * k + s, s * N_MM
+                cut = N_MM - SHARE if u < SHARED else N_MM
+                interleave("vector", x_grp[u][:, 0:cut, :], x_raw[k][:, :, lo:lo + cut])
+                if u < SHARED:
+                    interleave("scalar", x_grp[u][:, cut:N_MM, :], x_raw[k][:, :, lo + cut:lo + N_MM])
+            for s in range(UNITS):
+                u = UNITS * k + s
                 quantize(x_codes[u][:], x_scales[u][:], x_grp[u][:])
 
         def multiply(k):
@@ -112,7 +115,7 @@ def tile_rows_glin_relu_bias_kernel(tc, x, w, b, out):
                     for g in range(G):
                         rows = slice(g * ROWS, (g + 1) * ROWS)
                         nc.tensor.matmul_mx(
-                            out=acc(k, g, h)[:, s * N_MM:(s + 1) * N_MM],
+                            out=acc(k, g, h, s),
                             lhsT=w_codes[rows, h, :].bitcast(FP8X4),
                             lhsT_scale=w_scales[rows, h, :],
                             rhs=x_codes[u][rows, :].bitcast(FP8X4),
@@ -122,18 +125,26 @@ def tile_rows_glin_relu_bias_kernel(tc, x, w, b, out):
                         )
 
         def finish(engine, k, g, h):
-            column = bias[:, g * HALVES + h, 0:1]
-            if engine == "vector":
-                nc.vector.tensor_scalar(
-                    out=res[(k, h)][:, g], in0=acc(k, g, h), scalar1=column, scalar2=0.0, op0=ALU.add, op1=ALU.max
-                )
+            c = (g * HALVES + h) * BIAS_STEP
+            column = bias[:, c:c + 1]
+            if g == 0 and h == 0:
+                pieces = [(res[(k, h)][:, g, s * N_MM:(s + 1) * N_MM], acc(k, g, h, s)) for s in range(UNITS)]
             else:
-                nc.scalar.activation(out=res[(k, h)][:, g], in_=acc(k, g, h), func=ACT.Relu, bias=column)
+                lo = (k // 2) * STEP
+                pieces = [(res[(k, h)][:, g], banks[(g, h, k % 2)][:, lo:lo + STEP])]
+            for dst, src in pieces:
+                if engine == "vector":
+                    nc.vector.tensor_scalar(
+                        out=dst, in0=src, scalar1=column, scalar2=0.0, op0=ALU.add, op1=ALU.max
+                    )
+                else:
+                    nc.scalar.activation(out=dst, in_=src, func=ACT.Relu, bias=column)
 
         def store(k, h, lo, hi):
             nc.sync.dma_start(out=out_rows[:, h, lo:hi, k * STEP:(k + 1) * STEP], in_=res[(k, h)][:, lo:hi])
 
         prepare(0)
+        nc.vector.transpose(out=bias[:], in_=bias_rows[:])
         multiply(0)
         for k in range(STEPS):
             if k < last:

@@ -66,11 +66,11 @@ def tile_rows_glin_relu_bias_kernel(tc, x, w, b, out):
                 for parity in range(2):
                     banks[(g, h, parity)] = psum.tile([P, BANK], F32, name="acc%d%d%d" % (g, h, parity))
 
-        def acc(k, g, h, s):
-            if g == 0 and h == 0:
+        def acc(k, g, h, s, count):
+            if g == 1 and h == 0:
                 return banks[(g, h, s)][:, k * N_MM:(k + 1) * N_MM]
             lo = (k // 2) * STEP + s * N_MM
-            return banks[(g, h, k % 2)][:, lo:lo + N_MM]
+            return banks[(g, h, k % 2)][:, lo:lo + count * N_MM]
 
         nc.vector.memset(bias_rows[:], 0.0)
         nc.sync.dma_start(out=w_raw[:], in_=w_rows)
@@ -112,10 +112,10 @@ def tile_rows_glin_relu_bias_kernel(tc, x, w, b, out):
             for h in range(HALVES):
                 for s in range(UNITS):
                     u = UNITS * k + s
-                    for g in range(G):
+                    for g in ((1 - h, h) if s == 0 else (h, 1 - h)):
                         rows = slice(g * ROWS, (g + 1) * ROWS)
                         nc.tensor.matmul_mx(
-                            out=acc(k, g, h, s),
+                            out=acc(k, g, h, s, 1),
                             lhsT=w_codes[rows, h, :].bitcast(FP8X4),
                             lhsT_scale=w_scales[rows, h, :],
                             rhs=x_codes[u][rows, :].bitcast(FP8X4),
@@ -124,21 +124,15 @@ def tile_rows_glin_relu_bias_kernel(tc, x, w, b, out):
                             stop=True,
                         )
 
-        def finish(engine, k, g, h):
+        def finish(engine, k, g, h, s, count):
             c = (g * HALVES + h) * BIAS_STEP
             column = bias[:, c:c + 1]
-            if g == 0 and h == 0:
-                pieces = [(res[(k, h)][:, g, s * N_MM:(s + 1) * N_MM], acc(k, g, h, s)) for s in range(UNITS)]
+            dst = res[(k, h)][:, g, s * N_MM:(s + count) * N_MM]
+            src = acc(k, g, h, s, count)
+            if engine == "vector":
+                nc.vector.tensor_scalar(out=dst, in0=src, scalar1=column, scalar2=0.0, op0=ALU.add, op1=ALU.max)
             else:
-                lo = (k // 2) * STEP
-                pieces = [(res[(k, h)][:, g], banks[(g, h, k % 2)][:, lo:lo + STEP])]
-            for dst, src in pieces:
-                if engine == "vector":
-                    nc.vector.tensor_scalar(
-                        out=dst, in0=src, scalar1=column, scalar2=0.0, op0=ALU.add, op1=ALU.max
-                    )
-                else:
-                    nc.scalar.activation(out=dst, in_=src, func=ACT.Relu, bias=column)
+                nc.scalar.activation(out=dst, in_=src, func=ACT.Relu, bias=column)
 
         def store(k, h, lo, hi):
             nc.sync.dma_start(out=out_rows[:, h, lo:hi, k * STEP:(k + 1) * STEP], in_=res[(k, h)][:, lo:hi])
@@ -149,13 +143,16 @@ def tile_rows_glin_relu_bias_kernel(tc, x, w, b, out):
         for k in range(STEPS):
             if k < last:
                 prepare(k + 1)
-            for h in range(HALVES):
-                vector_free = k == last or (k == last - 1 and h == HALVES - 1)
-                finish("scalar", k, 0, h)
-                apart = k == 0 and h == 0
-                if apart:
-                    store(k, h, 0, 1)
-                finish("vector" if vector_free else "scalar", k, 1, h)
-                store(k, h, 1 if apart else 0, G)
+            helper = "vector" if k == last else "scalar"
+            finish(helper, k, 1, 0, 0, 1)
+            finish("scalar", k, 0, 0, 0, UNITS)
+            apart = k % 2 == 0
+            if apart:
+                store(k, 0, 0, 1)
+            finish(helper, k, 1, 0, 1, 1)
+            store(k, 0, 1 if apart else 0, G)
+            finish("scalar", k, 1, 1, 0, UNITS)
+            finish("vector" if k >= last - 1 else "scalar", k, 0, 1, 0, UNITS)
+            store(k, 1, 0, G)
             if k < last:
                 multiply(k + 1)

@@ -25,7 +25,7 @@ BANK = 512
 QUAD = 32
 BIAS_STEP = QUAD // (G * HALVES)
 PAIR = 2
-SHARED = 3
+SHARED = 2
 SHARE = 40
 MX_ALIGN = 64
 ROW_ALIGN = STEP * 4
@@ -63,11 +63,11 @@ def tile_rows_glin_relu_bias_kernel(tc, x, w, b, out):
         banks = {}
         for g in range(G):
             for h in range(HALVES):
-                for parity in range(2):
-                    banks[(g, h, parity)] = psum.tile([P, BANK], F32, name="acc%d%d%d" % (g, h, parity))
+                for place in range(2):
+                    banks[(g, h, place)] = psum.tile([P, BANK], F32, name="acc%d%d%d" % (g, h, place))
 
         def acc(k, g, h, s, count):
-            if g == 1 and h == 0:
+            if g != h:
                 return banks[(g, h, s)][:, k * N_MM:(k + 1) * N_MM]
             lo = (k // 2) * STEP + s * N_MM
             return banks[(g, h, k % 2)][:, lo:lo + count * N_MM]
@@ -100,9 +100,9 @@ def tile_rows_glin_relu_bias_kernel(tc, x, w, b, out):
         def prepare(k):
             for s in range(UNITS):
                 u, lo = UNITS * k + s, s * N_MM
-                cut = N_MM - SHARE if u < SHARED else N_MM
+                cut = N_MM - SHARE if k < SHARED else N_MM
                 interleave("vector", x_grp[u][:, 0:cut, :], x_raw[k][:, :, lo:lo + cut])
-                if u < SHARED:
+                if k < SHARED:
                     interleave("scalar", x_grp[u][:, cut:N_MM, :], x_raw[k][:, :, lo + cut:lo + N_MM])
             for s in range(UNITS):
                 u = UNITS * k + s
@@ -143,16 +143,16 @@ def tile_rows_glin_relu_bias_kernel(tc, x, w, b, out):
         for k in range(STEPS):
             if k < last:
                 prepare(k + 1)
-            helper = "vector" if k == last else "scalar"
-            finish(helper, k, 1, 0, 0, 1)
-            finish("scalar", k, 0, 0, 0, UNITS)
-            apart = k % 2 == 0
-            if apart:
-                store(k, 0, 0, 1)
-            finish(helper, k, 1, 0, 1, 1)
-            store(k, 0, 1 if apart else 0, G)
-            finish("scalar", k, 1, 1, 0, UNITS)
-            finish("vector" if k >= last - 1 else "scalar", k, 0, 1, 0, UNITS)
-            store(k, 1, 0, G)
+            for h in range(HALVES):
+                inner, outer = h, 1 - h
+                vector_free = k == last or (k == last - 1 and h == HALVES - 1)
+                helper = "vector" if vector_free else "scalar"
+                finish("vector" if k == 0 and h == 1 else helper, k, outer, h, 0, 1)
+                finish("scalar", k, inner, h, 0, UNITS)
+                apart = h == 0 and k % 2 == 0
+                if apart:
+                    store(k, h, inner, inner + 1)
+                finish(helper, k, outer, h, 1, 1)
+                store(k, h, outer if apart else 0, G)
             if k < last:
                 multiply(k + 1)

@@ -27,6 +27,7 @@ BIAS_STEP = QUAD // (G * HALVES)
 PAIR = 2
 SHARED = 2
 SHARE = 40
+BETWEEN = 2
 MX_ALIGN = 64
 ROW_ALIGN = STEP * 4
 W_ALIGN = PACK * M * 4
@@ -63,14 +64,11 @@ def tile_rows_glin_relu_bias_kernel(tc, x, w, b, out):
         banks = {}
         for g in range(G):
             for h in range(HALVES):
-                for place in range(2):
-                    banks[(g, h, place)] = psum.tile([P, BANK], F32, name="acc%d%d%d" % (g, h, place))
+                for s in range(UNITS):
+                    banks[(g, h, s)] = psum.tile([P, BANK], F32, name="acc%d%d%d" % (g, h, s))
 
-        def acc(k, g, h, s, count):
-            if g != h:
-                return banks[(g, h, s)][:, k * N_MM:(k + 1) * N_MM]
-            lo = (k // 2) * STEP + s * N_MM
-            return banks[(g, h, k % 2)][:, lo:lo + count * N_MM]
+        def acc(k, g, h, s):
+            return banks[(g, h, s)][:, k * N_MM:(k + 1) * N_MM]
 
         nc.vector.memset(bias_rows[:], 0.0)
         nc.sync.dma_start(out=w_raw[:], in_=w_rows)
@@ -97,38 +95,41 @@ def tile_rows_glin_relu_bias_kernel(tc, x, w, b, out):
         for h in range(HALVES):
             quantize(w_codes[:, h, :], w_scales[:, h, :], w_grp[:, h])
 
-        def prepare(k):
+        def copies(k):
             for s in range(UNITS):
                 u, lo = UNITS * k + s, s * N_MM
                 cut = N_MM - SHARE if k < SHARED else N_MM
                 interleave("vector", x_grp[u][:, 0:cut, :], x_raw[k][:, :, lo:lo + cut])
                 if k < SHARED:
                     interleave("scalar", x_grp[u][:, cut:N_MM, :], x_raw[k][:, :, lo + cut:lo + N_MM])
-            for s in range(UNITS):
-                u = UNITS * k + s
-                quantize(x_codes[u][:], x_scales[u][:], x_grp[u][:])
+
+        def quantize_unit(k, s):
+            u = UNITS * k + s
+            quantize(x_codes[u][:], x_scales[u][:], x_grp[u][:])
+
+        def passes(h):
+            return [(1 - h, 0), (h, 0), (h, 1), (1 - h, 1)]
 
         def multiply(k):
             for h in range(HALVES):
-                for s in range(UNITS):
+                for g, s in passes(h):
                     u = UNITS * k + s
-                    for g in ((1 - h, h) if s == 0 else (h, 1 - h)):
-                        rows = slice(g * ROWS, (g + 1) * ROWS)
-                        nc.tensor.matmul_mx(
-                            out=acc(k, g, h, s, 1),
-                            lhsT=w_codes[rows, h, :].bitcast(FP8X4),
-                            lhsT_scale=w_scales[rows, h, :],
-                            rhs=x_codes[u][rows, :].bitcast(FP8X4),
-                            rhs_scale=x_scales[u][rows, :],
-                            start=True,
-                            stop=True,
-                        )
+                    rows = slice(g * ROWS, (g + 1) * ROWS)
+                    nc.tensor.matmul_mx(
+                        out=acc(k, g, h, s),
+                        lhsT=w_codes[rows, h, :].bitcast(FP8X4),
+                        lhsT_scale=w_scales[rows, h, :],
+                        rhs=x_codes[u][rows, :].bitcast(FP8X4),
+                        rhs_scale=x_scales[u][rows, :],
+                        start=True,
+                        stop=True,
+                    )
 
-        def finish(engine, k, g, h, s, count):
+        def finish(engine, k, g, h, s):
             c = (g * HALVES + h) * BIAS_STEP
             column = bias[:, c:c + 1]
-            dst = res[(k, h)][:, g, s * N_MM:(s + count) * N_MM]
-            src = acc(k, g, h, s, count)
+            dst = res[(k, h)][:, g, s * N_MM:(s + 1) * N_MM]
+            src = acc(k, g, h, s)
             if engine == "vector":
                 nc.vector.tensor_scalar(out=dst, in0=src, scalar1=column, scalar2=0.0, op0=ALU.add, op1=ALU.max)
             else:
@@ -137,22 +138,28 @@ def tile_rows_glin_relu_bias_kernel(tc, x, w, b, out):
         def store(k, h, lo, hi):
             nc.sync.dma_start(out=out_rows[:, h, lo:hi, k * STEP:(k + 1) * STEP], in_=res[(k, h)][:, lo:hi])
 
-        prepare(0)
+        copies(0)
+        quantize_unit(0, 0)
+        quantize_unit(0, 1)
         nc.vector.transpose(out=bias[:], in_=bias_rows[:])
         multiply(0)
         for k in range(STEPS):
             if k < last:
-                prepare(k + 1)
+                copies(k + 1)
+                quantize_unit(k + 1, 0)
+                finish("vector", k, passes(0)[BETWEEN][0], 0, passes(0)[BETWEEN][1])
+                quantize_unit(k + 1, 1)
             for h in range(HALVES):
-                inner, outer = h, 1 - h
                 vector_free = k == last or (k == last - 1 and h == HALVES - 1)
-                helper = "vector" if vector_free else "scalar"
-                finish("vector" if k == 0 and h == 1 else helper, k, outer, h, 0, 1)
-                finish("scalar", k, inner, h, 0, UNITS)
-                apart = h == 0 and k % 2 == 0
-                if apart:
-                    store(k, h, inner, inner + 1)
-                finish(helper, k, outer, h, 1, 1)
-                store(k, h, outer if apart else 0, G)
+                for n, (g, s) in enumerate(passes(h)):
+                    if k < last and h == 0 and n == BETWEEN:
+                        pass
+                    elif (vector_free and n % 2 == 1) or (k == 0 and h == 1 and n == 0):
+                        finish("vector", k, g, h, s)
+                    else:
+                        finish("scalar", k, g, h, s)
+                    if k == 0 and h == 0 and n == 2:
+                        store(k, h, 0, 1)
+                store(k, h, 1 if k == 0 and h == 0 else 0, G)
             if k < last:
                 multiply(k + 1)

@@ -25,7 +25,8 @@ BANK = 512
 QUAD = 32
 BIAS_STEP = QUAD // (G * HALVES)
 PAIR = 2
-SHARED = 2
+SHARED = 4
+SINGLE = 4
 SHARE = 40
 BETWEEN = 2
 MX_ALIGN = 64
@@ -52,8 +53,14 @@ def tile_rows_glin_relu_bias_kernel(tc, x, w, b, out):
         w_scales = sb.tile([P, HALVES, P], U8, name="w_scales", align_bytes=MX_ALIGN)
         bias_rows = sb.tile([P, QUAD], F32, name="bias_rows", align_bytes=MX_ALIGN)
         bias = sb.tile([P, QUAD], F32, name="bias", align_bytes=MX_ALIGN)
-        x_raw = [sb.tile([P, PACK, STEP], F32, name="x_raw%d" % k, align_bytes=ROW_ALIGN) for k in range(STEPS)]
         units = range(STEPS * UNITS)
+        firsts = [u for u in units if u < SINGLE or u % UNITS == 0]
+        loads, x_raw = [], []
+        for u in firsts:
+            count = 1 if u < SINGLE else UNITS
+            landed = sb.tile([P, PACK, count * N_MM], F32, name="x_raw%d" % u, align_bytes=ROW_ALIGN)
+            loads.append((landed, x_rows[:, :, u * N_MM:(u + count) * N_MM]))
+            x_raw.extend(landed[:, :, s * N_MM:(s + 1) * N_MM] for s in range(count))
         x_grp = [sb.tile([P, N_MM, PACK], BF16, name="x_grp%d" % u, align_bytes=MX_ALIGN) for u in units]
         x_codes = [sb.tile([P, N_MM], U32, name="x_codes%d" % u, align_bytes=MX_ALIGN) for u in units]
         x_scales = [sb.tile([P, N_MM], U8, name="x_scales%d" % u, align_bytes=MX_ALIGN) for u in units]
@@ -71,10 +78,10 @@ def tile_rows_glin_relu_bias_kernel(tc, x, w, b, out):
             return banks[(g, h, s)][:, k * N_MM:(k + 1) * N_MM]
 
         nc.vector.memset(bias_rows[:], 0.0)
-        nc.sync.dma_start(out=w_raw[:], in_=w_rows)
-        for k in range(STEPS):
-            nc.sync.dma_start(out=x_raw[k][:], in_=x_rows[:, :, k * STEP:(k + 1) * STEP])
-            if k == 0:
+        for n, (landed, rows) in enumerate(loads):
+            nc.sync.dma_start(out=landed[:], in_=rows)
+            if n == 0:
+                nc.sync.dma_start(out=w_raw[:], in_=w_rows)
                 nc.sync.dma_start(out=bias_rows[0:P:BIAS_STEP], in_=b_rows)
 
         def interleave(engine, dst, src):
@@ -90,40 +97,36 @@ def tile_rows_glin_relu_bias_kernel(tc, x, w, b, out):
                 out=codes.bitcast(FP8X4), scales=scales, in_=grouped.rearrange("p n j -> p (n j)")
             )
 
-        interleave("scalar", w_grp[:, 1], w_raw[:, :, P:M])
-        interleave("vector", w_grp[:, 0], w_raw[:, :, 0:P])
-        for h in range(HALVES):
-            quantize(w_codes[:, h, :], w_scales[:, h, :], w_grp[:, h])
+        def shared(dst, src, share):
+            cut = N_MM - share
+            interleave("vector", dst[:, 0:cut, :], src[:, :, 0:cut])
+            if share:
+                interleave("scalar", dst[:, cut:N_MM, :], src[:, :, cut:N_MM])
 
-        def copies(k):
-            for s in range(UNITS):
-                u, lo = UNITS * k + s, s * N_MM
-                cut = N_MM - SHARE if k < SHARED else N_MM
-                interleave("vector", x_grp[u][:, 0:cut, :], x_raw[k][:, :, lo:lo + cut])
-                if k < SHARED:
-                    interleave("scalar", x_grp[u][:, cut:N_MM, :], x_raw[k][:, :, lo + cut:lo + N_MM])
+        def copy_unit(u):
+            shared(x_grp[u], x_raw[u], SHARE if 0 < u <= SHARED else 0)
 
-        def quantize_unit(k, s):
-            u = UNITS * k + s
+        def quantize_unit(u):
             quantize(x_codes[u][:], x_scales[u][:], x_grp[u][:])
 
-        def passes(h):
-            return [(1 - h, 0), (h, 0), (h, 1), (1 - h, 1)]
+        def passes(k):
+            if k == 0:
+                return [(g, h, s) for s in range(UNITS) for h in range(HALVES) for g in range(G)]
+            return [(g, h, s) for h in range(HALVES) for s in range(UNITS) for g in range(G)]
 
-        def multiply(k):
-            for h in range(HALVES):
-                for g, s in passes(h):
-                    u = UNITS * k + s
-                    rows = slice(g * ROWS, (g + 1) * ROWS)
-                    nc.tensor.matmul_mx(
-                        out=acc(k, g, h, s),
-                        lhsT=w_codes[rows, h, :].bitcast(FP8X4),
-                        lhsT_scale=w_scales[rows, h, :],
-                        rhs=x_codes[u][rows, :].bitcast(FP8X4),
-                        rhs_scale=x_scales[u][rows, :],
-                        start=True,
-                        stop=True,
-                    )
+        def multiply(k, lo, hi):
+            for g, h, s in passes(k)[lo:hi]:
+                u = UNITS * k + s
+                rows = slice(g * ROWS, (g + 1) * ROWS)
+                nc.tensor.matmul_mx(
+                    out=acc(k, g, h, s),
+                    lhsT=w_codes[rows, h, :].bitcast(FP8X4),
+                    lhsT_scale=w_scales[rows, h, :],
+                    rhs=x_codes[u][rows, :].bitcast(FP8X4),
+                    rhs_scale=x_scales[u][rows, :],
+                    start=True,
+                    stop=True,
+                )
 
         def finish(engine, k, g, h, s):
             c = (g * HALVES + h) * BIAS_STEP
@@ -135,31 +138,44 @@ def tile_rows_glin_relu_bias_kernel(tc, x, w, b, out):
             else:
                 nc.scalar.activation(out=dst, in_=src, func=ACT.Relu, bias=column)
 
-        def store(k, h, lo, hi):
-            nc.sync.dma_start(out=out_rows[:, h, lo:hi, k * STEP:(k + 1) * STEP], in_=res[(k, h)][:, lo:hi])
+        def store(k, h):
+            nc.sync.dma_start(out=out_rows[:, h, :, k * STEP:(k + 1) * STEP], in_=res[(k, h)][:])
 
-        copies(0)
-        quantize_unit(0, 0)
-        quantize_unit(0, 1)
+        def leave(engine, k, n):
+            g, h, s = passes(k)[n]
+            finish(engine, k, g, h, s)
+            if (g, s) == (G - 1, UNITS - 1):
+                store(k, h)
+
+        copy_unit(0)
+        quantize_unit(0)
+        for h in range(HALVES):
+            shared(w_grp[:, h], w_raw[:, :, h * P:(h + 1) * P], SHARE)
+        quantize(w_codes[:, 0, :], w_scales[:, 0, :], w_grp[:, 0])
+        copy_unit(1)
+        quantize(w_codes[:, 1, :], w_scales[:, 1, :], w_grp[:, 1])
         nc.vector.transpose(out=bias[:], in_=bias_rows[:])
-        multiply(0)
+        quantize_unit(1)
+        multiply(0, 0, 8)
+        copy_unit(2)
         for k in range(STEPS):
+            a, z = UNITS * (k + 1), UNITS * (k + 1) + 1
+            if k == 0:
+                leave("scalar", k, 0)
             if k < last:
-                copies(k + 1)
-                quantize_unit(k + 1, 0)
-                finish("vector", k, passes(0)[BETWEEN][0], 0, passes(0)[BETWEEN][1])
-                quantize_unit(k + 1, 1)
-            for h in range(HALVES):
-                vector_free = k == last or (k == last - 1 and h == HALVES - 1)
-                for n, (g, s) in enumerate(passes(h)):
-                    if k < last and h == 0 and n == BETWEEN:
-                        pass
-                    elif (vector_free and n % 2 == 1) or (k == 0 and h == 1 and n == 0):
-                        finish("vector", k, g, h, s)
-                    else:
-                        finish("scalar", k, g, h, s)
-                    if k == 0 and h == 0 and n == 2:
-                        store(k, h, 0, 1)
-                store(k, h, 1 if k == 0 and h == 0 else 0, G)
+                copy_unit(z)
+                quantize_unit(a)
+                leave("vector", k, BETWEEN)
+                quantize_unit(z)
+            for n in range(1 if k == 0 else 0, 8):
+                vector_free = k == last or (k == last - 1 and n >= 4)
+                if n == 7 and k < last - 1:
+                    copy_unit(z + 1)
+                if k < last and n == BETWEEN:
+                    pass
+                elif (vector_free and n % 2 == 1) or (k == 0 and n == BETWEEN + 1):
+                    leave("vector", k, n)
+                else:
+                    leave("scalar", k, n)
             if k < last:
-                multiply(k + 1)
+                multiply(k + 1, 0, 8)

@@ -25,8 +25,8 @@ BANK = 512
 QUAD = 32
 BIAS_STEP = QUAD // (G * HALVES)
 PAIR = 2
-SHARED = 4
-SINGLE = 4
+SHARED = 3
+SINGLE = 8
 SHARE = 40
 BETWEEN = 2
 MX_ALIGN = 64
@@ -39,7 +39,7 @@ def tile_rows_glin_relu_bias_kernel(tc, x, w, b, out):
     x_rows = x.rearrange("g (p j) n -> (g p) j n", j=PACK)
     w_rows = w.rearrange("g (p j) m -> (g p) j m", j=PACK)
     b_rows = b.rearrange("g (h u i) o -> u (g h) (i o)", h=HALVES, i=QUAD)
-    out_rows = out.rearrange("g (h q) n -> q h g n", h=HALVES)
+    out_rows = out.rearrange("g (h q) n -> q g h n", h=HALVES)
     last = STEPS - 1
 
     with ExitStack() as ctx:
@@ -65,9 +65,8 @@ def tile_rows_glin_relu_bias_kernel(tc, x, w, b, out):
         x_codes = [sb.tile([P, N_MM], U32, name="x_codes%d" % u, align_bytes=MX_ALIGN) for u in units]
         x_scales = [sb.tile([P, N_MM], U8, name="x_scales%d" % u, align_bytes=MX_ALIGN) for u in units]
         res = {}
-        for k in range(STEPS):
-            for h in range(HALVES):
-                res[(k, h)] = sb.tile([P, G, STEP], F32, name="res%d%d" % (k, h), align_bytes=ROW_ALIGN)
+        for u in units:
+            res[u] = sb.tile([P, G, HALVES, N_MM], F32, name="res%d" % u, align_bytes=ROW_ALIGN)
         banks = {}
         for g in range(G):
             for h in range(HALVES):
@@ -110,9 +109,7 @@ def tile_rows_glin_relu_bias_kernel(tc, x, w, b, out):
             quantize(x_codes[u][:], x_scales[u][:], x_grp[u][:])
 
         def passes(k):
-            if k == 0:
-                return [(g, h, s) for s in range(UNITS) for h in range(HALVES) for g in range(G)]
-            return [(g, h, s) for h in range(HALVES) for s in range(UNITS) for g in range(G)]
+            return [(g, h, s) for s in range(UNITS) for h in range(HALVES) for g in range(G)]
 
         def multiply(k, lo, hi):
             for g, h, s in passes(k)[lo:hi]:
@@ -131,21 +128,24 @@ def tile_rows_glin_relu_bias_kernel(tc, x, w, b, out):
         def finish(engine, k, g, h, s):
             c = (g * HALVES + h) * BIAS_STEP
             column = bias[:, c:c + 1]
-            dst = res[(k, h)][:, g, s * N_MM:(s + 1) * N_MM]
+            dst = res[UNITS * k + s][:, g, h]
             src = acc(k, g, h, s)
             if engine == "vector":
                 nc.vector.tensor_scalar(out=dst, in0=src, scalar1=column, scalar2=0.0, op0=ALU.add, op1=ALU.max)
             else:
                 nc.scalar.activation(out=dst, in_=src, func=ACT.Relu, bias=column)
 
-        def store(k, h):
-            nc.sync.dma_start(out=out_rows[:, h, :, k * STEP:(k + 1) * STEP], in_=res[(k, h)][:])
+        def store(u, lo, hi):
+            nc.sync.dma_start(out=out_rows[:, :, lo:hi, u * N_MM:(u + 1) * N_MM], in_=res[u][:, :, lo:hi])
 
         def leave(engine, k, n):
             g, h, s = passes(k)[n]
-            finish(engine, k, g, h, s)
-            if (g, s) == (G - 1, UNITS - 1):
-                store(k, h)
+            if engine:
+                finish(engine, k, g, h, s)
+            if g == G - 1 and k < last:
+                store(UNITS * k + s, h, h + 1)
+            elif (g, h) == (G - 1, HALVES - 1):
+                store(UNITS * k + s, 0, HALVES)
 
         copy_unit(0)
         quantize_unit(0)
@@ -162,18 +162,19 @@ def tile_rows_glin_relu_bias_kernel(tc, x, w, b, out):
             a, z = UNITS * (k + 1), UNITS * (k + 1) + 1
             if k == 0:
                 leave("scalar", k, 0)
+                leave("scalar", k, 1)
             if k < last:
                 copy_unit(z)
                 quantize_unit(a)
-                leave("vector", k, BETWEEN)
+                finish("vector", k, *passes(k)[BETWEEN])
                 quantize_unit(z)
-            for n in range(1 if k == 0 else 0, 8):
+            for n in range(2 if k == 0 else 0, 8):
                 vector_free = k == last or (k == last - 1 and n >= 4)
                 if n == 7 and k < last - 1:
                     copy_unit(z + 1)
                 if k < last and n == BETWEEN:
-                    pass
-                elif (vector_free and n % 2 == 1) or (k == 0 and n == BETWEEN + 1):
+                    leave(None, k, n)
+                elif vector_free and n % 2 == 1:
                     leave("vector", k, n)
                 else:
                     leave("scalar", k, n)

from contextlib import ExitStack

import concourse.mybir as mybir

G, D, M, N = 2, 256, 256, 1024
FLOPS = 2 * G * D * M * N

F32 = mybir.dt.float32
BF16 = mybir.dt.bfloat16
U32 = mybir.dt.uint32
U8 = mybir.dt.uint8
FP8X4 = mybir.dt.float8_e4m3fn_x4
ACT = mybir.ActivationFunctionType
ALU = mybir.AluOpType

P = 128
PACK = 4
ROWS = D // PACK
HALVES = M // P
N_MM = 128
UNITS = 2
STEP = UNITS * N_MM
STEPS = N // STEP
BANK = 512
QUAD = 32
BIAS_STEP = QUAD // (G * HALVES)
PAIR = 2
SHARED = 3
SINGLE = 8
SHARE = 40
BETWEEN = 2
MX_ALIGN = 64
ROW_ALIGN = STEP * 4
W_ALIGN = PACK * M * 4


def tile_rows_glin_relu_bias_kernel(tc, x, w, b, out):
    nc = tc.nc
    x_rows = x.rearrange("g (p j) n -> (g p) j n", j=PACK)
    w_rows = w.rearrange("g (p j) m -> (g p) j m", j=PACK)
    b_rows = b.rearrange("g (h u i) o -> u (g h) (i o)", h=HALVES, i=QUAD)
    out_rows = out.rearrange("g (h q) n -> q g h n", h=HALVES)
    last = STEPS - 1

    with ExitStack() as ctx:
        sb = ctx.enter_context(tc.tile_pool(name="sb", bufs=1))
        psum = ctx.enter_context(tc.psum_pool(name="psum", bufs=1))
        ctx.enter_context(tc.manual_schedule())

        w_raw = sb.tile([P, PACK, M], F32, name="w_raw", align_bytes=W_ALIGN)
        w_grp = sb.tile([P, HALVES, P, PACK], BF16, name="w_grp", align_bytes=MX_ALIGN)
        w_codes = sb.tile([P, HALVES, P], U32, name="w_codes", align_bytes=MX_ALIGN)
        w_scales = sb.tile([P, HALVES, P], U8, name="w_scales", align_bytes=MX_ALIGN)
        bias_rows = sb.tile([P, QUAD], F32, name="bias_rows", align_bytes=MX_ALIGN)
        bias = sb.tile([P, QUAD], F32, name="bias", align_bytes=MX_ALIGN)
        units = range(STEPS * UNITS)
        firsts = [u for u in units if u < SINGLE or u % UNITS == 0]
        loads, x_raw = [], []
        for u in firsts:
            count = 1 if u < SINGLE else UNITS
            landed = sb.tile([P, PACK, count * N_MM], F32, name="x_raw%d" % u, align_bytes=ROW_ALIGN)
            loads.append((landed, x_rows[:, :, u * N_MM:(u + count) * N_MM]))
            x_raw.extend(landed[:, :, s * N_MM:(s + 1) * N_MM] for s in range(count))
        x_grp = [sb.tile([P, N_MM, PACK], BF16, name="x_grp%d" % u, align_bytes=MX_ALIGN) for u in units]
        x_codes = [sb.tile([P, N_MM], U32, name="x_codes%d" % u, align_bytes=MX_ALIGN) for u in units]
        x_scales = [sb.tile([P, N_MM], U8, name="x_scales%d" % u, align_bytes=MX_ALIGN) for u in units]
        res = {}
        for u in units:
            res[u] = sb.tile([P, G, HALVES, N_MM], F32, name="res%d" % u, align_bytes=ROW_ALIGN)
        banks = {}
        for g in range(G):
            for h in range(HALVES):
                for s in range(UNITS):
                    banks[(g, h, s)] = psum.tile([P, BANK], F32, name="acc%d%d%d" % (g, h, s))

        def acc(k, g, h, s):
            return banks[(g, h, s)][:, k * N_MM:(k + 1) * N_MM]

        nc.vector.memset(bias_rows[:], 0.0)
        for n, (landed, rows) in enumerate(loads):
            nc.sync.dma_start(out=landed[:], in_=rows)
            if n == 0:
                nc.sync.dma_start(out=w_raw[:], in_=w_rows)
                nc.sync.dma_start(out=bias_rows[0:P:BIAS_STEP], in_=b_rows)

        def interleave(engine, dst, src):
            dst = dst.rearrange("p (a i) j -> p a j i", i=PAIR)
            src = src.rearrange("p j (a i) -> p a j i", i=PAIR)
            if engine == "vector":
                nc.vector.tensor_copy(out=dst, in_=src)
            else:
                nc.scalar.activation(out=dst, in_=src, func=ACT.Copy)

        def quantize(codes, scales, grouped):
            nc.vector.quantize_mx(
                out=codes.bitcast(FP8X4), scales=scales, in_=grouped.rearrange("p n j -> p (n j)")
            )

        def shared(dst, src, share):
            cut = N_MM - share
            interleave("vector", dst[:, 0:cut, :], src[:, :, 0:cut])
            if share:
                interleave("scalar", dst[:, cut:N_MM, :], src[:, :, cut:N_MM])

        def copy_unit(u):
            shared(x_grp[u], x_raw[u], SHARE if 0 < u <= SHARED else 0)

        def quantize_unit(u):
            quantize(x_codes[u][:], x_scales[u][:], x_grp[u][:])

        def passes(k):
            return [(g, h, s) for s in range(UNITS) for h in range(HALVES) for g in range(G)]

        def multiply(k, lo, hi):
            for g, h, s in passes(k)[lo:hi]:
                u = UNITS * k + s
                rows = slice(g * ROWS, (g + 1) * ROWS)
                nc.tensor.matmul_mx(
                    out=acc(k, g, h, s),
                    lhsT=w_codes[rows, h, :].bitcast(FP8X4),
                    lhsT_scale=w_scales[rows, h, :],
                    rhs=x_codes[u][rows, :].bitcast(FP8X4),
                    rhs_scale=x_scales[u][rows, :],
                    start=True,
                    stop=True,
                )

        def finish(engine, k, g, h, s):
            c = (g * HALVES + h) * BIAS_STEP
            column = bias[:, c:c + 1]
            dst = res[UNITS * k + s][:, g, h]
            src = acc(k, g, h, s)
            if engine == "vector":
                nc.vector.tensor_scalar(out=dst, in0=src, scalar1=column, scalar2=0.0, op0=ALU.add, op1=ALU.max)
            else:
                nc.scalar.activation(out=dst, in_=src, func=ACT.Relu, bias=column)

        def store(u, lo, hi):
            nc.sync.dma_start(out=out_rows[:, :, lo:hi, u * N_MM:(u + 1) * N_MM], in_=res[u][:, :, lo:hi])

        def leave(engine, k, n):
            g, h, s = passes(k)[n]
            if engine:
                finish(engine, k, g, h, s)
            if g == G - 1 and k < last:
                store(UNITS * k + s, h, h + 1)
            elif (g, h) == (G - 1, HALVES - 1):
                store(UNITS * k + s, 0, HALVES)

        copy_unit(0)
        quantize_unit(0)
        for h in range(HALVES):
            shared(w_grp[:, h], w_raw[:, :, h * P:(h + 1) * P], SHARE)
        quantize(w_codes[:, 0, :], w_scales[:, 0, :], w_grp[:, 0])
        copy_unit(1)
        quantize(w_codes[:, 1, :], w_scales[:, 1, :], w_grp[:, 1])
        nc.vector.transpose(out=bias[:], in_=bias_rows[:])
        quantize_unit(1)
        multiply(0, 0, 8)
        copy_unit(2)
        for k in range(STEPS):
            a, z = UNITS * (k + 1), UNITS * (k + 1) + 1
            if k == 0:
                leave("scalar", k, 0)
                leave("scalar", k, 1)
            if k < last:
                copy_unit(z)
                quantize_unit(a)
                finish("vector", k, *passes(k)[BETWEEN])
                quantize_unit(z)
            for n in range(2 if k == 0 else 0, 8):
                vector_free = k == last or (k == last - 1 and n >= 4)
                if n == 7 and k < last - 1:
                    copy_unit(z + 1)
                if k < last and n == BETWEEN:
                    leave(None, k, n)
                elif vector_free and n % 2 == 1:
                    leave("vector", k, n)
                else:
                    leave("scalar", k, n)
            if k < last:
                multiply(k + 1, 0, 8)
